import numpy as np
import ml_dtypes


def mxq(x, axis, fmt="e4m3"):
    dtype, down = {"e4m3": (ml_dtypes.float8_e4m3fn, 7), "e5m2": (ml_dtypes.float8_e5m2, 14)}[fmt]
    v = np.moveaxis(np.asarray(x, np.float32).astype(ml_dtypes.bfloat16).astype(np.float64), axis, -1)
    blocks = v.reshape(v.shape[:-1] + (-1, 32))
    amax = np.abs(blocks).max(-1, keepdims=True)
    byte = np.maximum(np.where(amax > 0, np.frexp(amax)[1] - 1 + 127, 0) - down, 1)
    scale = np.exp2(byte - 127.0)
    codes = (blocks / scale).astype(np.float32).astype(dtype).astype(np.float64)
    return np.moveaxis((codes * scale).reshape(v.shape), -1, axis)


WIDE = False


def mx_kscale(k):
    if not WIDE:
        return np.ones(k)
    levels = np.array([10, -10, 5, -5, 0])
    if k % 512:
        return np.exp2(np.random.permutation(np.resize(levels, k // 32))).repeat(32)
    a = np.empty((k // 512, 16))
    for p in range(k // 512):
        a[p, :8] = np.random.permutation(np.resize(levels, 8))
        for g in range(8):
            far = levels[np.abs(levels - a[p, g]) >= 10]
            a[p, g + 8] = far[np.random.randint(len(far))]
    return np.exp2(a.ravel()).repeat(32)


def f64(x):
    return np.asarray(x).astype(np.float64)


def striped(idx):
    return np.tile(idx.reshape(-1, 16).T, (8, 1)).astype(np.uint16)


def unstriped(offs):
    return offs[:16].T.reshape(-1).astype(np.int64)


E2M1 = np.array([0.0, 0.5, 1.0, 1.5, 2.0, 3.0, 4.0, 6.0, -0.0, -0.5, -1.0, -1.5, -2.0, -3.0, -4.0, -6.0])


def pack_weight(w, fmt):
    k, n = w.shape
    w = f64(np.asarray(w, np.float32).astype(ml_dtypes.bfloat16)).reshape(k // 32, 32, n)
    amax = np.abs(w).max(1)
    if fmt == "e4m3":
        byte = np.frexp(amax)[1] - 1 + 127 - 7
    else:
        mant, ex = np.frexp(amax / 6.0)
        byte = np.where(mant > 0.5, ex, ex - 1) + 127
    byte = np.clip(np.where(amax > 0, byte, 1), 1, 254)
    scaled = (w * np.exp2(127.0 - byte)[:, None, :]).reshape(k, n).astype(np.float32)
    by_word = np.ascontiguousarray(scaled.reshape(k // 512, 128, 4, n).transpose(0, 1, 3, 2))
    if fmt == "e4m3":
        words = by_word.astype(ml_dtypes.float8_e4m3fn).view(np.uint8)
    else:
        c = by_word.astype(ml_dtypes.float4_e2m1fn).view(np.uint8) & 0xF
        words = (c[..., 0::2] | (c[..., 1::2] << 4)).reshape(k // 512, 128, 2 * n)
    return np.ascontiguousarray(words), np.ascontiguousarray(byte.astype(np.uint8).reshape(k // 512, 16, n))


def unpack_weight(words, scales, fmt):
    g, _, n = scales.shape
    words = np.ascontiguousarray(words).reshape(g, 128, n, -1)
    if fmt == "e4m3":
        vals = words.view(ml_dtypes.float8_e4m3fn).astype(np.float64)
    else:
        nib = np.empty((g, 128, n, 4), np.uint8)
        nib[..., 0::2] = words & 0xF
        nib[..., 1::2] = words >> 4
        vals = E2M1[nib]
    vals = vals * np.repeat(np.exp2(scales.astype(np.float64) - 127.0), 8, axis=1)[..., None]
    return vals.transpose(0, 1, 3, 2).reshape(g * 512, n)


def gelu(v):
    return 0.5 * v * (1.0 + np.tanh(np.sqrt(2.0 / np.pi) * (v + 0.044715 * v**3)))


K, R, H, N, T, S, P = 1024, 512, 512, 384, 2048, 1024, 512

def setup_inputs():
    n = np.random.standard_normal
    s, s2, u = mx_kscale(K)[:, None], mx_kscale(R)[:, None], mx_kscale(H)[:, None]
    perm = np.random.permutation(T)
    tab_words, tab_scales = pack_weight(n((K, T)) * s, "e4m3")
    tab2_words, tab2_scales = pack_weight(n((R, T)) * s2, "e4m3")
    w1_words, w1_scales = pack_weight(1.2 * n((K, H)) / np.sqrt(K) / s, "e2m1")
    w4_words, w4_scales = pack_weight(1.2 * n((R, H)) / np.sqrt(R) / s2, "e4m3")
    w6_words, w6_scales = pack_weight(n((H, N)) / np.sqrt(H) / u, "e2m1")
    return {
        "tab_words": tab_words, "tab_scales": tab_scales,
        "tab2_words": tab2_words, "tab2_scales": tab2_scales,
        "offs": striped(np.random.permutation(T)[:S]), "offs2": striped(np.random.permutation(T)[:P]),
        "pos1": striped(np.random.permutation(S)[:P]),
        "offs3": striped(perm[:S]), "offs4": striped(perm[S:S + P]),
        "w1_words": w1_words, "w1_scales": w1_scales,
        "w2": (1.2 * n((K, H)) / np.sqrt(K) / s).astype(np.float32),
        "w3": (1.2 * n((R, H)) / np.sqrt(R) / s2).astype(np.float32),
        "w4_words": w4_words, "w4_scales": w4_scales,
        "gr": (np.exp(0.3 * n(H)) * u[:, 0]).astype(np.float32),
        "w5": (1.5 * n((H, N)) / np.sqrt(H) / u).astype(np.float32),
        "w6_words": w6_words, "w6_scales": w6_scales,
        "page1": n((N, T)).astype(np.float32),
        "wg1": np.exp(0.3 * n((128, S))).astype(np.float32), "wg2": np.exp(0.3 * n((128, P))).astype(np.float32)}

def reference(tab_words, tab_scales, tab2_words, tab2_scales, offs, offs2, pos1, offs3, offs4, w1_words, w1_scales, w2, w3, w4_words, w4_scales, gr, w5, w6_words, w6_scales, page1, wg1, wg2):
    v = unpack_weight(tab_words, tab_scales, "e4m3")[:, unstriped(offs)]
    v2 = unpack_weight(tab2_words, tab2_scales, "e4m3")[:, unstriped(offs2)]
    h1 = (unpack_weight(w1_words, w1_scales, "e2m1").T @ v) * (mxq(f64(w2), 0, "e4m3").T @ v)
    h2 = (mxq(f64(w3), 0, "e4m3").T @ v2) * (unpack_weight(w4_words, w4_scales, "e4m3").T @ v2)
    z = np.concatenate([np.tanh(h1), h2 + h1[:, unstriped(pos1)]], axis=1) * f64(gr)[:, None]
    zq = mxq(z, 0, "e4m3")
    y1 = mxq(f64(w5), 0, "e4m3").T @ zq[:, :S]
    y2 = unpack_weight(w6_words, w6_scales, "e2m1").T @ zq[:, S:]
    out = f64(page1).copy()
    out[:, unstriped(offs3)] = np.tile(f64(wg1), (N // 128, 1)) * y1
    out[:, unstriped(offs4)] = np.tile(f64(wg2), (N // 128, 1)) * y2
    return out

@@ -1,0 +1,323 @@
+from contextlib import ExitStack
+
+import concourse.mybir as mybir
+
+K, R, H, N, T, S, C = 1024, 512, 512, 384, 2048, 1024, 512
+FLOPS = 2 * (2 * K * H * S + 2 * R * H * C + H * N * (S + C))
+
+F32 = mybir.dt.float32
+BF16 = mybir.dt.bfloat16
+I32 = mybir.dt.int32
+U32 = mybir.dt.uint32
+U16 = mybir.dt.uint16
+U8 = mybir.dt.uint8
+FP8X4 = mybir.dt.float8_e4m3fn_x4
+FP4X4 = mybir.dt.float4_e2m1fn_x4
+MULT = mybir.AluOpType.mult
+ADD = mybir.AluOpType.add
+TANH = mybir.ActivationFunctionType.Tanh
+COPY = mybir.ActivationFunctionType.Copy
+
+P = 128
+PACK = 4
+K_PASS = P * PACK
+CHUNK = 256
+CHUNKS = S // CHUNK
+ROW_TILES = N // P
+STRIPE = 16
+W2_VECTOR_SHARE = 80
+
+
+def tile_list_repatriation_reserve_features_kernel(
+    tc, tab_words, tab_scales, tab2_words, tab2_scales, offs, offs2, pos1, offs3, offs4,
+    w1_words, w1_scales, w2, w3, w4_words, w4_scales, gr, w5, w6_words, w6_scales,
+    page1, wg1, wg2, out,
+):
+    nc = tc.nc
+    passes = K // K_PASS
+
+    with ExitStack() as ctx:
+        keep = ctx.enter_context(tc.tile_pool(name="keep", bufs=1))
+        ring = ctx.enter_context(tc.tile_pool(name="ring", bufs=2))
+        psum = ctx.enter_context(tc.psum_pool(name="psum", bufs=1))
+
+        def held(name, shape, dtype):
+            return keep.tile(shape, dtype, name=name, align_bytes=64)
+
+        def load_list(name, src):
+            tile = keep.tile(list(src.shape), U16, name=name)
+            nc.sync.dma_start(tile[:], src)
+            return tile
+
+        def load(name, src, dtype):
+            tile = held(name, list(src.shape), dtype)
+            nc.sync.dma_start(tile[:], src)
+            return tile
+
+        def zeroed_plane(name, src, engine):
+            tile = held(name, [P, src.shape[0], src.shape[2]], U8)
+            engine.memset(tile[:].bitcast(I32), 0)
+            return tile
+
+        def load_scales(tile, src, queue):
+            for q in range(4):
+                queue.dma_start(
+                    tile[32 * q : 32 * q + 4, :, :].bitcast(I32),
+                    src[:, 4 * q : 4 * q + 4, :].rearrange("a r c -> r a c").bitcast(I32),
+                )
+
+        def words32(src):
+            return src.rearrange("p c i -> p (c i)").bitcast(I32)
+
+        def rows4(src):
+            return src.rearrange("(p j) c -> p j c", j=PACK)
+
+        tab_plane = held("tab_plane", [P, T], U8)
+        nc.vector.memset(tab_plane[:].bitcast(I32), 0)
+        v_plane = [held("v_plane%d" % a, [P, S], U8) for a in range(passes)]
+        w1_plane_raw = zeroed_plane("w1_plane_raw", w1_scales, nc.vector)
+        nc.vector.memset(v_plane[1][:].bitcast(I32), 0)
+        tab2_plane = zeroed_plane("tab2_plane", tab2_scales, nc.vector)
+        w4_plane_raw = zeroed_plane("w4_plane_raw", w4_scales, nc.vector)
+        w6_plane = zeroed_plane("w6_plane", w6_scales, nc.vector)
+
+        tab_sb = [None] * passes
+        w2_raw = [None] * passes
+        for q in range(4):
+            nc.sync.dma_start(
+                tab_plane[32 * q : 32 * q + 4 * passes, :].bitcast(I32),
+                tab_scales[:, 4 * q : 4 * q + 4, :].bitcast(I32),
+            )
+        offs_sb = load_list("offs_sb", offs)
+        tab_sb[0] = load("tab_sb0", words32(tab_words[0]), I32)
+        w1_raw = held("w1_raw", [P, passes, 2 * H], U8)
+        nc.sync.dma_start(w1_raw[:].bitcast(I32), w1_words.rearrange("a p c -> p a c").bitcast(I32))
+        load_scales(w1_plane_raw, w1_scales, nc.sync)
+        tab_sb[1] = load("tab_sb1", words32(tab_words[1]), I32)
+        nc.vector.tensor_copy(v_plane[0][:], tab_plane[:].indirect(offs_sb[:]))
+        for q in range(4):
+            nc.sync.dma_start(
+                v_plane[1][32 * q : 32 * q + 4, :].bitcast(I32),
+                v_plane[0][32 * q + 4 : 32 * q + 8, :].bitcast(I32),
+            )
+        w2_raw[0] = load("w2_raw0", rows4(w2[0:K_PASS, :]), F32)
+        w2_raw[1] = load("w2_raw1", rows4(w2[K_PASS : 2 * K_PASS, :]), F32)
+        gr_sb = held("gr_sb", [P, PACK], F32)
+        nc.gpsimd.dma_start(gr_sb[:], gr.rearrange("(p t) -> p t", t=PACK))
+        w5_raw = load("w5_raw", rows4(w5), F32)
+        offs3_sb = load_list("offs3_sb", offs3)
+        wg1_sb = load("wg1_sb", wg1, F32)
+        page = [load("page%d" % n, page1[n * P : (n + 1) * P, :], F32) for n in range(ROW_TILES)]
+        offs2_sb = load_list("offs2_sb", offs2)
+        tab2_sb = load("tab2_sb", words32(tab2_words[0]), I32)
+        load_scales(tab2_plane, tab2_scales, nc.gpsimd)
+        w3_raw = load("w3_raw", rows4(w3), F32)
+        w4_raw = load("w4_raw", words32(w4_words[0]), I32)
+        load_scales(w4_plane_raw, w4_scales, nc.gpsimd)
+        pos1_sb = load_list("pos1_sb", pos1)
+        offs4_sb = load_list("offs4_sb", offs4)
+        wg2_sb = load("wg2_sb", wg2, F32)
+        w6_sb = held("w6_sb", [P, 2 * N], U8)
+        nc.sync.dma_start(w6_sb[:].bitcast(I32), w6_words[0].bitcast(I32))
+        load_scales(w6_plane, w6_scales, nc.gpsimd)
+
+        def quantize(name, grouped, width):
+            codes = held(name + "_codes", [P, width], U32)
+            plane = held(name + "_plane", [P, width], U8)
+            nc.vector.quantize_mx(out=codes[:].bitcast(FP8X4), scales=plane[:], in_=grouped)
+            return codes, plane
+
+        def quantize_dealt(name, raw, pieces, vector_share):
+            grouped = held(name + "_grouped", [P, PACK * H], BF16)
+            dst = grouped[:].rearrange("p (t m j) -> p m j t", t=PACK, j=PACK)
+            src = raw[:].rearrange("p j (m t) -> p m j t", t=PACK)
+            step = (P - vector_share) // pieces
+            for m0 in range(vector_share, P, step):
+                nc.scalar.copy(dst[:, m0 : m0 + step], src[:, m0 : m0 + step])
+            if vector_share:
+                nc.vector.tensor_copy(dst[:, :vector_share], src[:, :vector_share])
+            return quantize(name, grouped[:], H)
+
+        def interleave(grouped, planar, c0, c1):
+            dst = grouped[:].rearrange("p (c i j) -> p c j i", i=4, j=PACK)
+            src = planar[:].rearrange("p j (c i) -> p c j i", i=4)
+            nc.scalar.copy(dst[:, c0 // 4 : c1 // 4], src[:, c0 // 4 : c1 // 4])
+
+        v_codes = [held("v_codes%d" % a, [P, S], U32) for a in range(passes)]
+        nc.vector.tensor_copy(v_codes[0][:], tab_sb[0][:].bitcast(U32).indirect(offs_sb[:]))
+        w1_codes = held("w1_codes", [P, passes, 2 * H], U8)
+        nc.scalar.copy(
+            w1_codes[:].bitcast(U16).rearrange("p a (t m) -> p a t m", t=PACK),
+            w1_raw[:].bitcast(U16).rearrange("p a (m t) -> p a t m", t=PACK),
+        )
+        w1_plane = held("w1_plane", [P, passes, H], U8)
+        nc.vector.tensor_copy(
+            w1_plane[:].rearrange("p a (t m) -> p a t m", t=PACK),
+            w1_plane_raw[:].rearrange("p a (m t) -> p a t m", t=PACK),
+        )
+        for c in range(CHUNKS):
+            entries = offs_sb[:, c * CHUNK // STRIPE : (c + 1) * CHUNK // STRIPE]
+            nc.vector.tensor_copy(
+                v_codes[1][:, c * CHUNK : (c + 1) * CHUNK], tab_sb[1][:].bitcast(U32).indirect(entries)
+            )
+        w2_q = [quantize_dealt("w2_%d" % a, w2_raw[a], 1, W2_VECTOR_SHARE) for a in range(passes)]
+
+        h1 = [held("h1_%d" % t, [P, S], F32) for t in range(PACK)]
+
+        def first_stage(c):
+            cols = slice(c * CHUNK, (c + 1) * CHUNK)
+            for half in range(2):
+                left = psum.tile([P, 2, CHUNK], F32, tag="left", bufs=3, name="left")
+                right = psum.tile([P, 2, CHUNK], F32, tag="right", bufs=3, name="right")
+                for a in range(passes):
+                    for u in range(2):
+                        t = 2 * half + u
+                        nc.tensor.matmul_mx(
+                            left[:, u, :],
+                            lhsT=w1_codes[:, a, 2 * P * t : 2 * P * (t + 1)].bitcast(FP4X4),
+                            lhsT_scale=w1_plane[:, a, P * t : P * (t + 1)],
+                            rhs=v_codes[a][:, cols].bitcast(FP8X4),
+                            rhs_scale=v_plane[a][:, cols],
+                            start=(a == 0 and u == 0),
+                            stop=(a == passes - 1 and u == 1),
+                        )
+                for a in range(passes):
+                    for u in range(2):
+                        t = 2 * half + u
+                        nc.tensor.matmul_mx(
+                            right[:, u, :],
+                            lhsT=w2_q[a][0][:, P * t : P * (t + 1)].bitcast(FP8X4),
+                            lhsT_scale=w2_q[a][1][:, P * t : P * (t + 1)],
+                            rhs=v_codes[a][:, cols].bitcast(FP8X4),
+                            rhs_scale=v_plane[a][:, cols],
+                            start=(a == 0 and u == 0),
+                            stop=(a == passes - 1 and u == 1),
+                        )
+                left_sb = ring.tile([P, 2, CHUNK], F32, tag="left_sb", bufs=2, name="left_sb")
+                nc.scalar.copy(left_sb[:], left[:])
+                for u in range(2):
+                    nc.vector.tensor_tensor(h1[2 * half + u][:, cols], right[:, u, :], left_sb[:, u, :], MULT)
+
+        def gain_round_quantize(name, values, width):
+            planar = ring.tile([P, PACK, width], BF16, tag="planar", name="planar")
+            for t in range(PACK):
+                nc.scalar.activation(planar[:, t, :], values[t], COPY, scale=gr_sb[:, t : t + 1])
+            grouped = ring.tile([P, PACK * width], BF16, tag="handover", bufs=1, name="grouped", align_bytes=64)
+            interleave(grouped, planar, 0, width)
+            return quantize(name, grouped[:], width)
+
+        def z1_chunk(c):
+            cols = slice(c * CHUNK, (c + 1) * CHUNK)
+            bent = ring.tile([P, PACK, CHUNK], F32, tag="bent", name="bent")
+            for t in range(PACK):
+                nc.scalar.activation(bent[:, t, :], h1[t][:, cols], TANH)
+            if c == 0:
+                grouped = ring.tile([P, PACK * CHUNK], BF16, tag="handover", bufs=1, name="grouped", align_bytes=64)
+                nc.vector.tensor_tensor(
+                    grouped[:].rearrange("p (c i j) -> p c j i", i=4, j=PACK),
+                    bent[:].rearrange("p j (c i) -> p c j i", i=4),
+                    gr_sb[:].unsqueeze(1).unsqueeze(3).to_broadcast([P, CHUNK // 4, PACK, 4]),
+                    MULT,
+                )
+                return quantize("z1_0", grouped[:], CHUNK)
+            return gain_round_quantize("z1_%d" % c, [bent[:, t, :] for t in range(PACK)], CHUNK)
+
+        def second_stage(n, z_q, weight, weight_plane, gains, entries, held_back):
+            width = gains.shape[1]
+            y = psum.tile([P, width], F32, tag="y", bufs=2, name="y")
+            nc.tensor.matmul_mx(
+                y[:], lhsT=weight, lhsT_scale=weight_plane,
+                rhs=z_q[0][:].bitcast(FP8X4), rhs_scale=z_q[1][:], start=True, stop=True,
+            )
+            if held_back:
+                y_sb = ring.tile([P, width], F32, tag="handover", bufs=1, name="y_held", align_bytes=64)
+            else:
+                y_sb = ring.tile([P, width], F32, tag="y_sb", bufs=3, name="y_sb")
+            nc.scalar.copy(y_sb[:], y[:])
+            nc.vector.tensor_tensor(page[n][:].indirect(entries), y_sb[:], gains, MULT)
+
+        def y1_tile(c, n):
+            second_stage(
+                n, z1_q[c], w5_q[n][0][:].bitcast(FP8X4), w5_q[n][1][:],
+                wg1_sb[:, c * CHUNK : (c + 1) * CHUNK],
+                offs3_sb[:, c * CHUNK // STRIPE : (c + 1) * CHUNK // STRIPE], n == ROW_TILES - 1,
+            )
+
+        def quantize_w5(n):
+            grouped = held("w5_grouped%d" % n, [P, PACK * P], BF16)
+            nc.scalar.copy(
+                grouped[:].rearrange("p (c i j) -> p c j i", i=4, j=PACK),
+                w5_raw[:, :, P * n : P * (n + 1)].rearrange("p j (c i) -> p c j i", i=4),
+            )
+            return quantize("w5_%d" % n, grouped[:], P)
+
+        z1_q = [None] * CHUNKS
+        w5_q = [None] * ROW_TILES
+        first_stage(0)
+        z1_q[0] = z1_chunk(0)
+        w5_q[0] = quantize_w5(0)
+        first_stage(1)
+        y1_tile(0, 0)
+        w5_q[1] = quantize_w5(1)
+        y1_tile(0, 1)
+        z1_q[1] = z1_chunk(1)
+        w5_q[2] = quantize_w5(2)
+        y1_tile(0, 2)
+        first_stage(2)
+        y1_tile(1, 0)
+        y1_tile(1, 1)
+        z1_q[2] = z1_chunk(2)
+        y1_tile(1, 2)
+        first_stage(3)
+        y1_tile(2, 0)
+        y1_tile(2, 1)
+
+        v2_codes = held("v2_codes", [P, C], U32)
+        v2_plane = held("v2_plane", [P, C], U8)
+        nc.vector.tensor_copy(v2_codes[:], tab2_sb[:].bitcast(U32).indirect(offs2_sb[:]))
+        nc.vector.tensor_copy(v2_plane[:], tab2_plane[:, 0, :].indirect(offs2_sb[:]))
+
+        w3_q = quantize_dealt("w3", w3_raw, 4, 0)
+        w4_codes = held("w4_codes", [P, H], I32)
+        nc.gpsimd.tensor_copy(
+            w4_codes[:].rearrange("p (t m) -> p m t", t=PACK),
+            w4_raw[:].rearrange("p (m t) -> p m t", t=PACK),
+        )
+        w4_plane = held("w4_plane", [P, H], U8)
+        nc.gpsimd.tensor_copy(
+            w4_plane[:].rearrange("p (t m) -> p t m", t=PACK),
+            w4_plane_raw[:, 0, :].rearrange("p (m t) -> p t m", t=PACK),
+        )
+        h2 = held("h2", [P, PACK, C], F32)
+        for t in range(PACK):
+            left = psum.tile([P, C], F32, tag="left", bufs=3, name="left")
+            right = psum.tile([P, C], F32, tag="right", bufs=3, name="right")
+            cols = slice(P * t, P * (t + 1))
+            nc.tensor.matmul_mx(
+                left[:], lhsT=w3_q[0][:, cols].bitcast(FP8X4), lhsT_scale=w3_q[1][:, cols],
+                rhs=v2_codes[:].bitcast(FP8X4), rhs_scale=v2_plane[:], start=True, stop=True,
+            )
+            nc.tensor.matmul_mx(
+                right[:], lhsT=w4_codes[:, cols].bitcast(FP8X4), lhsT_scale=w4_plane[:, cols],
+                rhs=v2_codes[:].bitcast(FP8X4), rhs_scale=v2_plane[:], start=True, stop=True,
+            )
+            left_sb = ring.tile([P, C], F32, tag="left_sb", bufs=2, name="left_sb")
+            nc.scalar.copy(left_sb[:], left[:])
+            nc.vector.tensor_tensor(h2[:, t, :], right[:], left_sb[:], MULT)
+
+        z1_q[3] = z1_chunk(3)
+        joined = held("joined", [P, PACK, C], F32)
+        for t in range(PACK):
+            nc.vector.tensor_tensor(joined[:, t, :], h1[t][:].indirect(pos1_sb[:]), h2[:, t, :], ADD)
+        y1_tile(2, 2)
+        y1_tile(3, 0)
+        y1_tile(3, 1)
+        z2_q = gain_round_quantize("z2", [joined[:, t, :] for t in range(PACK)], C)
+        y1_tile(3, 2)
+        for n in range(ROW_TILES):
+            second_stage(
+                n, z2_q, w6_sb[:, 2 * P * n : 2 * P * (n + 1)].bitcast(FP4X4), w6_plane[:, 0, P * n : P * (n + 1)],
+                wg2_sb[:], offs4_sb[:], False,
+            )
+        for n in range(ROW_TILES):
+            nc.sync.dma_start(out[n * P : (n + 1) * P, :], page[n][:])

@@ -25,7 +25,7 @@ CHUNK = 256
 CHUNKS = S // CHUNK
 ROW_TILES = N // P
 STRIPE = 16
-W2_VECTOR_SHARE = 80
+W2_VECTOR_SHARE = (48, 80)
 
 
 def tile_list_repatriation_reserve_features_kernel(
@@ -92,7 +92,7 @@ def tile_list_repatriation_reserve_features_kernel(
         tab_sb[0] = load("tab_sb0", words32(tab_words[0]), I32)
         w1_raw = held("w1_raw", [P, passes, 2 * H], U8)
         nc.sync.dma_start(w1_raw[:].bitcast(I32), w1_words.rearrange("a p c -> p a c").bitcast(I32))
-        load_scales(w1_plane_raw, w1_scales, nc.sync)
+        load_scales(w1_plane_raw, w1_scales, nc.gpsimd)
         tab_sb[1] = load("tab_sb1", words32(tab_words[1]), I32)
         nc.vector.tensor_copy(v_plane[0][:], tab_plane[:].indirect(offs_sb[:]))
         for q in range(4):
@@ -100,18 +100,25 @@ def tile_list_repatriation_reserve_features_kernel(
                 v_plane[1][32 * q : 32 * q + 4, :].bitcast(I32),
                 v_plane[0][32 * q + 4 : 32 * q + 8, :].bitcast(I32),
             )
-        w2_raw[0] = load("w2_raw0", rows4(w2[0:K_PASS, :]), F32)
-        w2_raw[1] = load("w2_raw1", rows4(w2[K_PASS : 2 * K_PASS, :]), F32)
+        for a in range(passes):
+            w2_raw[a] = ring.tile([P, PACK, H], F32, tag="stage", bufs=2, name="w2_raw")
+            nc.sync.dma_start(w2_raw[a][:], rows4(w2[a * K_PASS : (a + 1) * K_PASS, :]))
         gr_sb = held("gr_sb", [P, PACK], F32)
         nc.gpsimd.dma_start(gr_sb[:], gr.rearrange("(p t) -> p t", t=PACK))
-        w5_raw = load("w5_raw", rows4(w5), F32)
+        w5_first = ring.tile([P, PACK, P], F32, tag="w5_slot", bufs=1, name="w5_first")
+        nc.sync.dma_start(w5_first[:], rows4(w5[:, :P]))
         offs3_sb = load_list("offs3_sb", offs3)
         wg1_sb = load("wg1_sb", wg1, F32)
-        page = [load("page%d" % n, page1[n * P : (n + 1) * P, :], F32) for n in range(ROW_TILES)]
+        page = [None] * ROW_TILES
+        page[0] = load("page0", page1[:P, :], F32)
+        w5_rest = load("w5_rest", rows4(w5[:, P:]), F32)
+        for n in range(1, ROW_TILES):
+            page[n] = load("page%d" % n, page1[n * P : (n + 1) * P, :], F32)
+        w3_raw = ring.tile([P, PACK, H], F32, tag="w3_slot", bufs=1, name="w3_raw")
+        nc.sync.dma_start(w3_raw[:], rows4(w3))
         offs2_sb = load_list("offs2_sb", offs2)
         tab2_sb = load("tab2_sb", words32(tab2_words[0]), I32)
         load_scales(tab2_plane, tab2_scales, nc.gpsimd)
-        w3_raw = load("w3_raw", rows4(w3), F32)
         w4_raw = load("w4_raw", words32(w4_words[0]), I32)
         load_scales(w4_plane_raw, w4_scales, nc.gpsimd)
         pos1_sb = load_list("pos1_sb", pos1)
@@ -160,7 +167,7 @@ def tile_list_repatriation_reserve_features_kernel(
             nc.vector.tensor_copy(
                 v_codes[1][:, c * CHUNK : (c + 1) * CHUNK], tab_sb[1][:].bitcast(U32).indirect(entries)
             )
-        w2_q = [quantize_dealt("w2_%d" % a, w2_raw[a], 1, W2_VECTOR_SHARE) for a in range(passes)]
+        w2_q = [quantize_dealt("w2_%d" % a, w2_raw[a], 1, W2_VECTOR_SHARE[a]) for a in range(passes)]
 
         h1 = [held("h1_%d" % t, [P, S], F32) for t in range(PACK)]
 
@@ -193,16 +200,21 @@ def tile_list_repatriation_reserve_features_kernel(
                             start=(a == 0 and u == 0),
                             stop=(a == passes - 1 and u == 1),
                         )
-                left_sb = ring.tile([P, 2, CHUNK], F32, tag="left_sb", bufs=2, name="left_sb")
+                if c == 0:
+                    left_sb = ring.tile([P, 2, CHUNK], F32, tag="stage", bufs=2, name="left_sb")
+                elif (c, half) == (1, 0):
+                    left_sb = ring.tile([P, 2, CHUNK], F32, tag="w5_slot", bufs=1, name="left_sb")
+                else:
+                    left_sb = ring.tile([P, 2, CHUNK], F32, tag="left_sb", bufs=2, name="left_sb")
                 nc.scalar.copy(left_sb[:], left[:])
                 for u in range(2):
                     nc.vector.tensor_tensor(h1[2 * half + u][:, cols], right[:, u, :], left_sb[:, u, :], MULT)
 
-        def gain_round_quantize(name, values, width):
-            planar = ring.tile([P, PACK, width], BF16, tag="planar", name="planar")
+        def gain_round_quantize(name, values, width, slot):
+            planar = ring.tile([P, PACK, width], BF16, tag=slot, bufs=1, name="planar")
             for t in range(PACK):
                 nc.scalar.activation(planar[:, t, :], values[t], COPY, scale=gr_sb[:, t : t + 1])
-            grouped = ring.tile([P, PACK * width], BF16, tag="handover", bufs=1, name="grouped", align_bytes=64)
+            grouped = ring.tile([P, PACK * width], BF16, tag="grouped", name="grouped", align_bytes=64)
             interleave(grouped, planar, 0, width)
             return quantize(name, grouped[:], width)
 
@@ -212,7 +224,7 @@ def tile_list_repatriation_reserve_features_kernel(
             for t in range(PACK):
                 nc.scalar.activation(bent[:, t, :], h1[t][:, cols], TANH)
             if c == 0:
-                grouped = ring.tile([P, PACK * CHUNK], BF16, tag="handover", bufs=1, name="grouped", align_bytes=64)
+                grouped = ring.tile([P, PACK * CHUNK], BF16, tag="grouped", name="grouped", align_bytes=64)
                 nc.vector.tensor_tensor(
                     grouped[:].rearrange("p (c i j) -> p c j i", i=4, j=PACK),
                     bent[:].rearrange("p j (c i) -> p c j i", i=4),
@@ -220,34 +232,32 @@ def tile_list_repatriation_reserve_features_kernel(
                     MULT,
                 )
                 return quantize("z1_0", grouped[:], CHUNK)
-            return gain_round_quantize("z1_%d" % c, [bent[:, t, :] for t in range(PACK)], CHUNK)
+            return gain_round_quantize("z1_%d" % c, [bent[:, t, :] for t in range(PACK)], CHUNK, "handover")
 
-        def second_stage(n, z_q, weight, weight_plane, gains, entries, held_back):
+        def second_stage(n, z_q, weight, weight_plane, gains, entries, slot):
             width = gains.shape[1]
             y = psum.tile([P, width], F32, tag="y", bufs=2, name="y")
             nc.tensor.matmul_mx(
                 y[:], lhsT=weight, lhsT_scale=weight_plane,
                 rhs=z_q[0][:].bitcast(FP8X4), rhs_scale=z_q[1][:], start=True, stop=True,
             )
-            if held_back:
-                y_sb = ring.tile([P, width], F32, tag="handover", bufs=1, name="y_held", align_bytes=64)
-            else:
-                y_sb = ring.tile([P, width], F32, tag="y_sb", bufs=3, name="y_sb")
+            y_sb = ring.tile([P, width], F32, tag=slot, bufs=3 if slot == "y_sb" else 1, name=slot)
             nc.scalar.copy(y_sb[:], y[:])
             nc.vector.tensor_tensor(page[n][:].indirect(entries), y_sb[:], gains, MULT)
 
-        def y1_tile(c, n):
+        def y1_tile(c, n, slot="y_sb"):
             second_stage(
                 n, z1_q[c], w5_q[n][0][:].bitcast(FP8X4), w5_q[n][1][:],
                 wg1_sb[:, c * CHUNK : (c + 1) * CHUNK],
-                offs3_sb[:, c * CHUNK // STRIPE : (c + 1) * CHUNK // STRIPE], n == ROW_TILES - 1,
+                offs3_sb[:, c * CHUNK // STRIPE : (c + 1) * CHUNK // STRIPE], slot,
             )
 
         def quantize_w5(n):
+            raw = w5_first[:] if n == 0 else w5_rest[:, :, P * (n - 1) : P * n]
             grouped = held("w5_grouped%d" % n, [P, PACK * P], BF16)
             nc.scalar.copy(
                 grouped[:].rearrange("p (c i j) -> p c j i", i=4, j=PACK),
-                w5_raw[:, :, P * n : P * (n + 1)].rearrange("p j (c i) -> p c j i", i=4),
+                raw.rearrange("p j (c i) -> p c j i", i=4),
             )
             return quantize("w5_%d" % n, grouped[:], P)
 
@@ -260,17 +270,16 @@ def tile_list_repatriation_reserve_features_kernel(
         y1_tile(0, 0)
         w5_q[1] = quantize_w5(1)
         y1_tile(0, 1)
+        first_stage(2)
         z1_q[1] = z1_chunk(1)
         w5_q[2] = quantize_w5(2)
-        y1_tile(0, 2)
-        first_stage(2)
+        y1_tile(0, 2, "handover")
         y1_tile(1, 0)
         y1_tile(1, 1)
         z1_q[2] = z1_chunk(2)
-        y1_tile(1, 2)
+        y1_tile(1, 2, "handover")
         first_stage(3)
         y1_tile(2, 0)
-        y1_tile(2, 1)
 
         v2_codes = held("v2_codes", [P, C], U32)
         v2_plane = held("v2_plane", [P, C], U8)
@@ -278,10 +287,11 @@ def tile_list_repatriation_reserve_features_kernel(
         nc.vector.tensor_copy(v2_plane[:], tab2_plane[:, 0, :].indirect(offs2_sb[:]))
 
         w3_q = quantize_dealt("w3", w3_raw, 4, 0)
-        w4_codes = held("w4_codes", [P, H], I32)
-        nc.gpsimd.tensor_copy(
+        y1_tile(2, 1, "w3_slot")
+        w4_codes = held("w4_codes", [P, H], U32)
+        nc.scalar.copy(
             w4_codes[:].rearrange("p (t m) -> p m t", t=PACK),
-            w4_raw[:].rearrange("p (m t) -> p m t", t=PACK),
+            w4_raw[:].bitcast(U32).rearrange("p (m t) -> p m t", t=PACK),
         )
         w4_plane = held("w4_plane", [P, H], U8)
         nc.gpsimd.tensor_copy(
@@ -309,15 +319,15 @@ def tile_list_repatriation_reserve_features_kernel(
         joined = held("joined", [P, PACK, C], F32)
         for t in range(PACK):
             nc.vector.tensor_tensor(joined[:, t, :], h1[t][:].indirect(pos1_sb[:]), h2[:, t, :], ADD)
-        y1_tile(2, 2)
+        y1_tile(2, 2, "handover")
         y1_tile(3, 0)
         y1_tile(3, 1)
-        z2_q = gain_round_quantize("z2", [joined[:, t, :] for t in range(PACK)], C)
-        y1_tile(3, 2)
+        z2_q = gain_round_quantize("z2", [joined[:, t, :] for t in range(PACK)], C, "last_handover")
+        y1_tile(3, 2, "last_handover")
         for n in range(ROW_TILES):
             second_stage(
                 n, z2_q, w6_sb[:, 2 * P * n : 2 * P * (n + 1)].bitcast(FP4X4), w6_plane[:, 0, P * n : P * (n + 1)],
-                wg2_sb[:], offs4_sb[:], False,
+                wg2_sb[:], offs4_sb[:], "y_sb",
             )
         for n in range(ROW_TILES):
             nc.sync.dma_start(out[n * P : (n + 1) * P, :], page[n][:])

@@ -25,7 +25,7 @@ CHUNK = 256
 CHUNKS = S // CHUNK
 ROW_TILES = N // P
 STRIPE = 16
-W2_VECTOR_SHARE = (48, 80)
+W2_VECTOR_SHARE = (80, 80)
 
 
 def tile_list_repatriation_reserve_features_kernel(
@@ -72,61 +72,59 @@ def tile_list_repatriation_reserve_features_kernel(
         def rows4(src):
             return src.rearrange("(p j) c -> p j c", j=PACK)
 
-        tab_plane = held("tab_plane", [P, T], U8)
-        nc.vector.memset(tab_plane[:].bitcast(I32), 0)
-        v_plane = [held("v_plane%d" % a, [P, S], U8) for a in range(passes)]
-        w1_plane_raw = zeroed_plane("w1_plane_raw", w1_scales, nc.vector)
-        nc.vector.memset(v_plane[1][:].bitcast(I32), 0)
-        tab2_plane = zeroed_plane("tab2_plane", tab2_scales, nc.vector)
-        w4_plane_raw = zeroed_plane("w4_plane_raw", w4_scales, nc.vector)
-        w6_plane = zeroed_plane("w6_plane", w6_scales, nc.vector)
+        tab_rows = held("tab_rows", [P, T], U8)
+        nc.vector.memset(tab_rows[32:64, :].bitcast(I32), 0)
+        nc.vector.memset(tab_rows[64:, :].bitcast(I32), 0)
+        w1_plane_raw = zeroed_plane("w1_plane_raw", w1_scales, nc.gpsimd)
+        v_plane = held("v_plane", [P, passes, S], U8)
+        nc.gpsimd.memset(v_plane[:].bitcast(I32), 0)
+        tab2_plane = zeroed_plane("tab2_plane", tab2_scales, nc.gpsimd)
+        w4_plane_raw = zeroed_plane("w4_plane_raw", w4_scales, nc.gpsimd)
+        w6_plane = zeroed_plane("w6_plane", w6_scales, nc.gpsimd)
 
         tab_sb = [None] * passes
         w2_raw = [None] * passes
-        for q in range(4):
-            nc.sync.dma_start(
-                tab_plane[32 * q : 32 * q + 4 * passes, :].bitcast(I32),
-                tab_scales[:, 4 * q : 4 * q + 4, :].bitcast(I32),
-            )
+        nc.sync.dma_start(tab_rows[:32, :].bitcast(I32), tab_scales.rearrange("a g t -> g a t").bitcast(I32))
         offs_sb = load_list("offs_sb", offs)
         tab_sb[0] = load("tab_sb0", words32(tab_words[0]), I32)
         w1_raw = held("w1_raw", [P, passes, 2 * H], U8)
         nc.sync.dma_start(w1_raw[:].bitcast(I32), w1_words.rearrange("a p c -> p a c").bitcast(I32))
-        load_scales(w1_plane_raw, w1_scales, nc.gpsimd)
+        load_scales(w1_plane_raw, w1_scales, nc.sync)
         tab_sb[1] = load("tab_sb1", words32(tab_words[1]), I32)
-        nc.vector.tensor_copy(v_plane[0][:], tab_plane[:].indirect(offs_sb[:]))
+        v_rows = held("v_rows", [P, S], U8)
+        nc.vector.tensor_copy(v_rows[:], tab_rows[:].indirect(offs_sb[:]))
         for q in range(4):
             nc.sync.dma_start(
-                v_plane[1][32 * q : 32 * q + 4, :].bitcast(I32),
-                v_plane[0][32 * q + 4 : 32 * q + 8, :].bitcast(I32),
+                v_plane[32 * q : 32 * q + 4, :, :].bitcast(I32), v_rows[8 * q : 8 * q + 8, :].bitcast(I32)
             )
         for a in range(passes):
             w2_raw[a] = ring.tile([P, PACK, H], F32, tag="stage", bufs=2, name="w2_raw")
             nc.sync.dma_start(w2_raw[a][:], rows4(w2[a * K_PASS : (a + 1) * K_PASS, :]))
-        gr_sb = held("gr_sb", [P, PACK], F32)
-        nc.gpsimd.dma_start(gr_sb[:], gr.rearrange("(p t) -> p t", t=PACK))
         w5_first = ring.tile([P, PACK, P], F32, tag="w5_slot", bufs=1, name="w5_first")
         nc.sync.dma_start(w5_first[:], rows4(w5[:, :P]))
+        gr_sb = held("gr_sb", [P, PACK], F32)
+        nc.sync.dma_start(gr_sb[:], gr.rearrange("(p t) -> p t", t=PACK))
         offs3_sb = load_list("offs3_sb", offs3)
         wg1_sb = load("wg1_sb", wg1, F32)
+        w5_rest = load("w5_rest", rows4(w5[:, P:]), F32)
         page = [None] * ROW_TILES
         page[0] = load("page0", page1[:P, :], F32)
-        w5_rest = load("w5_rest", rows4(w5[:, P:]), F32)
-        for n in range(1, ROW_TILES):
-            page[n] = load("page%d" % n, page1[n * P : (n + 1) * P, :], F32)
+        page[1] = load("page1", page1[P : 2 * P, :], F32)
+        page[2] = load("page2", page1[2 * P :, :], F32)
         w3_raw = ring.tile([P, PACK, H], F32, tag="w3_slot", bufs=1, name="w3_raw")
         nc.sync.dma_start(w3_raw[:], rows4(w3))
         offs2_sb = load_list("offs2_sb", offs2)
-        tab2_sb = load("tab2_sb", words32(tab2_words[0]), I32)
-        load_scales(tab2_plane, tab2_scales, nc.gpsimd)
+        load_scales(tab2_plane, tab2_scales, nc.sync)
+        tab2_sb = ring.tile([P, T], I32, tag="tab2_slot", bufs=1, name="tab2_sb")
+        nc.sync.dma_start(tab2_sb[:], words32(tab2_words[0]))
         w4_raw = load("w4_raw", words32(w4_words[0]), I32)
-        load_scales(w4_plane_raw, w4_scales, nc.gpsimd)
+        load_scales(w4_plane_raw, w4_scales, nc.sync)
         pos1_sb = load_list("pos1_sb", pos1)
         offs4_sb = load_list("offs4_sb", offs4)
         wg2_sb = load("wg2_sb", wg2, F32)
         w6_sb = held("w6_sb", [P, 2 * N], U8)
         nc.sync.dma_start(w6_sb[:].bitcast(I32), w6_words[0].bitcast(I32))
-        load_scales(w6_plane, w6_scales, nc.gpsimd)
+        load_scales(w6_plane, w6_scales, nc.sync)
 
         def quantize(name, grouped, width):
             codes = held(name + "_codes", [P, width], U32)
@@ -158,7 +156,7 @@ def tile_list_repatriation_reserve_features_kernel(
             w1_raw[:].bitcast(U16).rearrange("p a (m t) -> p a t m", t=PACK),
         )
         w1_plane = held("w1_plane", [P, passes, H], U8)
-        nc.vector.tensor_copy(
+        nc.gpsimd.tensor_copy(
             w1_plane[:].rearrange("p a (t m) -> p a t m", t=PACK),
             w1_plane_raw[:].rearrange("p a (m t) -> p a t m", t=PACK),
         )
@@ -173,6 +171,7 @@ def tile_list_repatriation_reserve_features_kernel(
 
         def first_stage(c):
             cols = slice(c * CHUNK, (c + 1) * CHUNK)
+            both_sb = ring.tile([P, PACK, CHUNK], F32, tag="stage", bufs=2, name="both_sb")
             for half in range(2):
                 left = psum.tile([P, 2, CHUNK], F32, tag="left", bufs=3, name="left")
                 right = psum.tile([P, 2, CHUNK], F32, tag="right", bufs=3, name="right")
@@ -184,7 +183,7 @@ def tile_list_repatriation_reserve_features_kernel(
                             lhsT=w1_codes[:, a, 2 * P * t : 2 * P * (t + 1)].bitcast(FP4X4),
                             lhsT_scale=w1_plane[:, a, P * t : P * (t + 1)],
                             rhs=v_codes[a][:, cols].bitcast(FP8X4),
-                            rhs_scale=v_plane[a][:, cols],
+                            rhs_scale=v_plane[:, a, cols],
                             start=(a == 0 and u == 0),
                             stop=(a == passes - 1 and u == 1),
                         )
@@ -196,17 +195,12 @@ def tile_list_repatriation_reserve_features_kernel(
                             lhsT=w2_q[a][0][:, P * t : P * (t + 1)].bitcast(FP8X4),
                             lhsT_scale=w2_q[a][1][:, P * t : P * (t + 1)],
                             rhs=v_codes[a][:, cols].bitcast(FP8X4),
-                            rhs_scale=v_plane[a][:, cols],
+                            rhs_scale=v_plane[:, a, cols],
                             start=(a == 0 and u == 0),
                             stop=(a == passes - 1 and u == 1),
                         )
-                if c == 0:
-                    left_sb = ring.tile([P, 2, CHUNK], F32, tag="stage", bufs=2, name="left_sb")
-                elif (c, half) == (1, 0):
-                    left_sb = ring.tile([P, 2, CHUNK], F32, tag="w5_slot", bufs=1, name="left_sb")
-                else:
-                    left_sb = ring.tile([P, 2, CHUNK], F32, tag="left_sb", bufs=2, name="left_sb")
-                nc.scalar.copy(left_sb[:], left[:])
+                left_sb = both_sb[:, 2 * half : 2 * half + 2, :]
+                nc.scalar.copy(left_sb, left[:])
                 for u in range(2):
                     nc.vector.tensor_tensor(h1[2 * half + u][:, cols], right[:, u, :], left_sb[:, u, :], MULT)
 
@@ -263,31 +257,32 @@ def tile_list_repatriation_reserve_features_kernel(
 
         z1_q = [None] * CHUNKS
         w5_q = [None] * ROW_TILES
+        w5_q[0] = quantize_w5(0)
         first_stage(0)
         z1_q[0] = z1_chunk(0)
-        w5_q[0] = quantize_w5(0)
         first_stage(1)
-        y1_tile(0, 0)
         w5_q[1] = quantize_w5(1)
+        y1_tile(0, 0)
+        w5_q[2] = quantize_w5(2)
         y1_tile(0, 1)
         first_stage(2)
+        first_stage(3)
         z1_q[1] = z1_chunk(1)
-        w5_q[2] = quantize_w5(2)
         y1_tile(0, 2, "handover")
         y1_tile(1, 0)
         y1_tile(1, 1)
         z1_q[2] = z1_chunk(2)
         y1_tile(1, 2, "handover")
-        first_stage(3)
         y1_tile(2, 0)
 
+        w3_q = quantize_dealt("w3", w3_raw, 4, 0)
+        z1_q[3] = z1_chunk(3)
         v2_codes = held("v2_codes", [P, C], U32)
         v2_plane = held("v2_plane", [P, C], U8)
         nc.vector.tensor_copy(v2_codes[:], tab2_sb[:].bitcast(U32).indirect(offs2_sb[:]))
         nc.vector.tensor_copy(v2_plane[:], tab2_plane[:, 0, :].indirect(offs2_sb[:]))
 
-        w3_q = quantize_dealt("w3", w3_raw, 4, 0)
-        y1_tile(2, 1, "w3_slot")
+        y1_tile(2, 1, "tab2_slot")
         w4_codes = held("w4_codes", [P, H], U32)
         nc.scalar.copy(
             w4_codes[:].rearrange("p (t m) -> p m t", t=PACK),
@@ -298,7 +293,7 @@ def tile_list_repatriation_reserve_features_kernel(
             w4_plane[:].rearrange("p (t m) -> p t m", t=PACK),
             w4_plane_raw[:, 0, :].rearrange("p (m t) -> p t m", t=PACK),
         )
-        h2 = held("h2", [P, PACK, C], F32)
+        h2 = [ring.tile([P, C], F32, tag="h2_%d" % t, bufs=1, name="h2") for t in range(PACK)]
         for t in range(PACK):
             left = psum.tile([P, C], F32, tag="left", bufs=3, name="left")
             right = psum.tile([P, C], F32, tag="right", bufs=3, name="right")
@@ -313,15 +308,14 @@ def tile_list_repatriation_reserve_features_kernel(
             )
             left_sb = ring.tile([P, C], F32, tag="left_sb", bufs=2, name="left_sb")
             nc.scalar.copy(left_sb[:], left[:])
-            nc.vector.tensor_tensor(h2[:, t, :], right[:], left_sb[:], MULT)
+            nc.vector.tensor_tensor(h2[t][:], right[:], left_sb[:], MULT)
 
-        z1_q[3] = z1_chunk(3)
         joined = held("joined", [P, PACK, C], F32)
         for t in range(PACK):
-            nc.vector.tensor_tensor(joined[:, t, :], h1[t][:].indirect(pos1_sb[:]), h2[:, t, :], ADD)
-        y1_tile(2, 2, "handover")
-        y1_tile(3, 0)
-        y1_tile(3, 1)
+            nc.vector.tensor_tensor(joined[:, t, :], h1[t][:].indirect(pos1_sb[:]), h2[t][:], ADD)
+        y1_tile(2, 2, "h2_0")
+        y1_tile(3, 0, "h2_1")
+        y1_tile(3, 1, "h2_2")
         z2_q = gain_round_quantize("z2", [joined[:, t, :] for t in range(PACK)], C, "last_handover")
         y1_tile(3, 2, "last_handover")
         for n in range(ROW_TILES):

@@ -21,11 +21,17 @@ COPY = mybir.ActivationFunctionType.Copy
 P = 128
 PACK = 4
 K_PASS = P * PACK
+PASSES = K // K_PASS
+QUADRANT = 32
+QUADRANTS = P // QUADRANT
+SCALE_ROWS = 4
+PAIR = 2
+PAIRS = PACK // PAIR
 CHUNK = 256
 CHUNKS = S // CHUNK
 ROW_TILES = N // P
 STRIPE = 16
-W2_VECTOR_SHARE = (80, 80)
+RUN = 4
 
 
 def tile_list_repatriation_reserve_features_kernel(
@@ -34,11 +40,10 @@ def tile_list_repatriation_reserve_features_kernel(
     page1, wg1, wg2, out,
 ):
     nc = tc.nc
-    passes = K // K_PASS
 
     with ExitStack() as ctx:
         keep = ctx.enter_context(tc.tile_pool(name="keep", bufs=1))
-        ring = ctx.enter_context(tc.tile_pool(name="ring", bufs=2))
+        ring = ctx.enter_context(tc.tile_pool(name="ring", bufs=1))
         psum = ctx.enter_context(tc.psum_pool(name="psum", bufs=1))
 
         def held(name, shape, dtype):
@@ -54,212 +59,223 @@ def tile_list_repatriation_reserve_features_kernel(
             nc.sync.dma_start(tile[:], src)
             return tile
 
-        def zeroed_plane(name, src, engine):
-            tile = held(name, [P, src.shape[0], src.shape[2]], U8)
-            engine.memset(tile[:].bitcast(I32), 0)
+        def zeroed_planes(name, passes, columns):
+            tile = held(name, [P, passes, columns], U8)
+            nc.gpsimd.memset(tile[:].bitcast(I32), 0)
             return tile
 
-        def load_scales(tile, src, queue):
-            for q in range(4):
-                queue.dma_start(
-                    tile[32 * q : 32 * q + 4, :, :].bitcast(I32),
-                    src[:, 4 * q : 4 * q + 4, :].rearrange("a r c -> r a c").bitcast(I32),
+        def load_planes(tile, scales):
+            for q in range(QUADRANTS):
+                nc.sync.dma_start(
+                    tile[QUADRANT * q : QUADRANT * q + SCALE_ROWS, :, :].bitcast(I32),
+                    scales[:, SCALE_ROWS * q : SCALE_ROWS * (q + 1), :].rearrange("a r c -> r a c").bitcast(I32),
                 )
 
-        def words32(src):
+        def as_words(src):
             return src.rearrange("p c i -> p (c i)").bitcast(I32)
 
-        def rows4(src):
+        def four_rows_a_partition(src):
             return src.rearrange("(p j) c -> p j c", j=PACK)
 
-        tab_rows = held("tab_rows", [P, T], U8)
-        nc.vector.memset(tab_rows[32:64, :].bitcast(I32), 0)
-        nc.vector.memset(tab_rows[64:, :].bitcast(I32), 0)
-        w1_plane_raw = zeroed_plane("w1_plane_raw", w1_scales, nc.gpsimd)
-        v_plane = held("v_plane", [P, passes, S], U8)
-        nc.gpsimd.memset(v_plane[:].bitcast(I32), 0)
-        tab2_plane = zeroed_plane("tab2_plane", tab2_scales, nc.gpsimd)
-        w4_plane_raw = zeroed_plane("w4_plane_raw", w4_scales, nc.gpsimd)
-        w6_plane = zeroed_plane("w6_plane", w6_scales, nc.gpsimd)
+        def chunk_columns(c):
+            return slice(c * CHUNK, (c + 1) * CHUNK)
 
-        tab_sb = [None] * passes
-        w2_raw = [None] * passes
-        nc.sync.dma_start(tab_rows[:32, :].bitcast(I32), tab_scales.rearrange("a g t -> g a t").bitcast(I32))
+        def chunk_entries(list_tile, c):
+            return list_tile[:, c * CHUNK // STRIPE : (c + 1) * CHUNK // STRIPE]
+
+        tab_rows = held("tab_rows", [P, T], U8)
+        nc.vector.memset(tab_rows[QUADRANT : 2 * QUADRANT, :].bitcast(I32), 0)
+        nc.vector.memset(tab_rows[2 * QUADRANT :, :].bitcast(I32), 0)
+        w1_plane_raw = zeroed_planes("w1_plane_raw", PASSES, H)
+        v_plane = zeroed_planes("v_plane", PASSES, S)
+        tab2_plane = zeroed_planes("tab2_plane", 1, T)
+        w4_plane_raw = zeroed_planes("w4_plane_raw", 1, H)
+        w6_plane = zeroed_planes("w6_plane", 1, N)
+
+        nc.sync.dma_start(tab_rows[:QUADRANT, :].bitcast(I32), tab_scales.rearrange("a g t -> g a t").bitcast(I32))
         offs_sb = load_list("offs_sb", offs)
-        tab_sb[0] = load("tab_sb0", words32(tab_words[0]), I32)
-        w1_raw = held("w1_raw", [P, passes, 2 * H], U8)
+        tab_pass0 = load("tab_pass0", as_words(tab_words[0]), I32)
+        w1_raw = held("w1_raw", [P, PASSES, 2 * H], U8)
         nc.sync.dma_start(w1_raw[:].bitcast(I32), w1_words.rearrange("a p c -> p a c").bitcast(I32))
-        load_scales(w1_plane_raw, w1_scales, nc.sync)
-        tab_sb[1] = load("tab_sb1", words32(tab_words[1]), I32)
+        load_planes(w1_plane_raw, w1_scales)
+        tab_pass1 = load("tab_pass1", as_words(tab_words[1]), I32)
+
         v_rows = held("v_rows", [P, S], U8)
         nc.vector.tensor_copy(v_rows[:], tab_rows[:].indirect(offs_sb[:]))
-        for q in range(4):
+        rows_a_quadrant = SCALE_ROWS * PASSES
+        for q in range(QUADRANTS):
             nc.sync.dma_start(
-                v_plane[32 * q : 32 * q + 4, :, :].bitcast(I32), v_rows[8 * q : 8 * q + 8, :].bitcast(I32)
+                v_plane[QUADRANT * q : QUADRANT * q + SCALE_ROWS, :, :].bitcast(I32),
+                v_rows[rows_a_quadrant * q : rows_a_quadrant * (q + 1), :].bitcast(I32),
             )
-        for a in range(passes):
-            w2_raw[a] = ring.tile([P, PACK, H], F32, tag="stage", bufs=2, name="w2_raw")
-            nc.sync.dma_start(w2_raw[a][:], rows4(w2[a * K_PASS : (a + 1) * K_PASS, :]))
-        w5_first = ring.tile([P, PACK, P], F32, tag="w5_slot", bufs=1, name="w5_first")
-        nc.sync.dma_start(w5_first[:], rows4(w5[:, :P]))
-        gr_sb = held("gr_sb", [P, PACK], F32)
-        nc.sync.dma_start(gr_sb[:], gr.rearrange("(p t) -> p t", t=PACK))
+
+        w2_raw = [ring.tile([P, PACK, H], F32, tag="after_w2", bufs=PASSES, name="w2_raw") for a in range(PASSES)]
+        for a in range(PASSES):
+            nc.sync.dma_start(w2_raw[a][:], four_rows_a_partition(w2[a * K_PASS : (a + 1) * K_PASS, :]))
+        w5_first = load("w5_first", four_rows_a_partition(w5[:, :P]), F32)
+        gr_sb = load("gr_sb", gr.rearrange("(p t) -> p t", t=PACK), F32)
         offs3_sb = load_list("offs3_sb", offs3)
         wg1_sb = load("wg1_sb", wg1, F32)
-        w5_rest = load("w5_rest", rows4(w5[:, P:]), F32)
-        page = [None] * ROW_TILES
-        page[0] = load("page0", page1[:P, :], F32)
-        page[1] = load("page1", page1[P : 2 * P, :], F32)
-        page[2] = load("page2", page1[2 * P :, :], F32)
-        w3_raw = ring.tile([P, PACK, H], F32, tag="w3_slot", bufs=1, name="w3_raw")
-        nc.sync.dma_start(w3_raw[:], rows4(w3))
+        w5_rest = load("w5_rest", four_rows_a_partition(w5[:, P:]), F32)
+        page = [load("page%d" % n, page1[n * P : (n + 1) * P, :], F32) for n in range(ROW_TILES)]
+        w3_raw = load("w3_raw", four_rows_a_partition(w3), F32)
         offs2_sb = load_list("offs2_sb", offs2)
-        load_scales(tab2_plane, tab2_scales, nc.sync)
-        tab2_sb = ring.tile([P, T], I32, tag="tab2_slot", bufs=1, name="tab2_sb")
-        nc.sync.dma_start(tab2_sb[:], words32(tab2_words[0]))
-        w4_raw = load("w4_raw", words32(w4_words[0]), I32)
-        load_scales(w4_plane_raw, w4_scales, nc.sync)
+        load_planes(tab2_plane, tab2_scales)
+        tab2_sb = ring.tile([P, T], I32, tag="after_tab2", name="tab2_sb")
+        nc.sync.dma_start(tab2_sb[:], as_words(tab2_words[0]))
+        w4_raw = load("w4_raw", as_words(w4_words[0]), I32)
+        load_planes(w4_plane_raw, w4_scales)
         pos1_sb = load_list("pos1_sb", pos1)
         offs4_sb = load_list("offs4_sb", offs4)
         wg2_sb = load("wg2_sb", wg2, F32)
         w6_sb = held("w6_sb", [P, 2 * N], U8)
         nc.sync.dma_start(w6_sb[:].bitcast(I32), w6_words[0].bitcast(I32))
-        load_scales(w6_plane, w6_scales, nc.sync)
+        load_planes(w6_plane, w6_scales)
 
         def quantize(name, grouped, width):
             codes = held(name + "_codes", [P, width], U32)
             plane = held(name + "_plane", [P, width], U8)
-            nc.vector.quantize_mx(out=codes[:].bitcast(FP8X4), scales=plane[:], in_=grouped)
+            nc.vector.quantize_mx(out=codes[:].bitcast(FP8X4), scales=plane[:], in_=grouped[:])
             return codes, plane
 
-        def quantize_dealt(name, raw, pieces, vector_share):
-            grouped = held(name + "_grouped", [P, PACK * H], BF16)
-            dst = grouped[:].rearrange("p (t m j) -> p m j t", t=PACK, j=PACK)
-            src = raw[:].rearrange("p j (m t) -> p m j t", t=PACK)
-            step = (P - vector_share) // pieces
-            for m0 in range(vector_share, P, step):
-                nc.scalar.copy(dst[:, m0 : m0 + step], src[:, m0 : m0 + step])
-            if vector_share:
-                nc.vector.tensor_copy(dst[:, :vector_share], src[:, :vector_share])
-            return quantize(name, grouped[:], H)
+        def interleaved_view(grouped):
+            return grouped[:].rearrange("p (c i j) -> p c j i", i=RUN, j=PACK)
 
-        def interleave(grouped, planar, c0, c1):
-            dst = grouped[:].rearrange("p (c i j) -> p c j i", i=4, j=PACK)
-            src = planar[:].rearrange("p j (c i) -> p c j i", i=4)
-            nc.scalar.copy(dst[:, c0 // 4 : c1 // 4], src[:, c0 // 4 : c1 // 4])
+        def planar_view(planar):
+            return planar.rearrange("p j (c i) -> p c j i", i=RUN)
 
-        v_codes = [held("v_codes%d" % a, [P, S], U32) for a in range(passes)]
-        nc.vector.tensor_copy(v_codes[0][:], tab_sb[0][:].bitcast(U32).indirect(offs_sb[:]))
-        w1_codes = held("w1_codes", [P, passes, 2 * H], U8)
+        def quantize_dealt_pair(name, raw, pair, copy, pieces):
+            grouped = held(name + "_grouped", [P, PACK * PAIR * P], BF16)
+            dst = grouped[:].rearrange("p (u m j) -> p m j u", u=PAIR, j=PACK)
+            src = raw[:].rearrange("p j (m t) -> p m j t", t=PACK)[:, :, :, PAIR * pair : PAIR * (pair + 1)]
+            step = P // pieces
+            for m0 in range(0, P, step):
+                copy(dst[:, m0 : m0 + step], src[:, m0 : m0 + step])
+            return quantize(name, grouped, PAIR * P)
+
+        def quantize_w5(n):
+            raw = w5_first[:] if n == 0 else w5_rest[:, :, P * (n - 1) : P * n]
+            grouped = held("w5_grouped%d" % n, [P, PACK * P], BF16)
+            nc.scalar.copy(interleaved_view(grouped), planar_view(raw))
+            return quantize("w5_%d" % n, grouped, P)
+
+        v_codes = [held("v_codes%d" % a, [P, S], U32) for a in range(PASSES)]
+        nc.vector.tensor_copy(v_codes[0][:], tab_pass0[:].bitcast(U32).indirect(offs_sb[:]))
+        w1_codes = held("w1_codes", [P, PASSES, 2 * H], U8)
         nc.scalar.copy(
             w1_codes[:].bitcast(U16).rearrange("p a (t m) -> p a t m", t=PACK),
             w1_raw[:].bitcast(U16).rearrange("p a (m t) -> p a t m", t=PACK),
         )
-        w1_plane = held("w1_plane", [P, passes, H], U8)
+        w1_plane = held("w1_plane", [P, PASSES, H], U8)
         nc.gpsimd.tensor_copy(
             w1_plane[:].rearrange("p a (t m) -> p a t m", t=PACK),
             w1_plane_raw[:].rearrange("p a (m t) -> p a t m", t=PACK),
         )
         for c in range(CHUNKS):
-            entries = offs_sb[:, c * CHUNK // STRIPE : (c + 1) * CHUNK // STRIPE]
             nc.vector.tensor_copy(
-                v_codes[1][:, c * CHUNK : (c + 1) * CHUNK], tab_sb[1][:].bitcast(U32).indirect(entries)
+                v_codes[1][:, chunk_columns(c)], tab_pass1[:].bitcast(U32).indirect(chunk_entries(offs_sb, c))
             )
-        w2_q = [quantize_dealt("w2_%d" % a, w2_raw[a], 1, W2_VECTOR_SHARE[a]) for a in range(passes)]
+        w2_copies = (
+            (nc.vector.tensor_copy, nc.scalar.copy),
+            (nc.vector.tensor_copy, nc.vector.tensor_copy),
+        )
+        w2_q = [
+            [quantize_dealt_pair("w2_%d_%d" % (a, pair), w2_raw[a], pair, w2_copies[a][pair], 1) for pair in range(PAIRS)]
+            for a in range(PASSES)
+        ]
 
         h1 = [held("h1_%d" % t, [P, S], F32) for t in range(PACK)]
 
         def first_stage(c):
-            cols = slice(c * CHUNK, (c + 1) * CHUNK)
-            both_sb = ring.tile([P, PACK, CHUNK], F32, tag="stage", bufs=2, name="both_sb")
-            for half in range(2):
-                left = psum.tile([P, 2, CHUNK], F32, tag="left", bufs=3, name="left")
-                right = psum.tile([P, 2, CHUNK], F32, tag="right", bufs=3, name="right")
-                for a in range(passes):
-                    for u in range(2):
-                        t = 2 * half + u
+            cols = chunk_columns(c)
+            w1_sums_sb = ring.tile([P, PACK, CHUNK], F32, tag="after_w2", bufs=PASSES, name="w1_sums_sb")
+            for pair in range(PAIRS):
+                w1_sums = psum.tile([P, PAIR, CHUNK], F32, tag="left", bufs=3, name="w1_sums")
+                w2_sums = psum.tile([P, PAIR, CHUNK], F32, tag="right", bufs=3, name="w2_sums")
+                for a in range(PASSES):
+                    for u in range(PAIR):
+                        t = PAIR * pair + u
                         nc.tensor.matmul_mx(
-                            left[:, u, :],
+                            w1_sums[:, u, :],
                             lhsT=w1_codes[:, a, 2 * P * t : 2 * P * (t + 1)].bitcast(FP4X4),
                             lhsT_scale=w1_plane[:, a, P * t : P * (t + 1)],
                             rhs=v_codes[a][:, cols].bitcast(FP8X4),
                             rhs_scale=v_plane[:, a, cols],
                             start=(a == 0 and u == 0),
-                            stop=(a == passes - 1 and u == 1),
+                            stop=(a == PASSES - 1 and u == PAIR - 1),
                         )
-                for a in range(passes):
-                    for u in range(2):
-                        t = 2 * half + u
+                for a in range(PASSES):
+                    codes, plane = w2_q[a][pair]
+                    for u in range(PAIR):
                         nc.tensor.matmul_mx(
-                            right[:, u, :],
-                            lhsT=w2_q[a][0][:, P * t : P * (t + 1)].bitcast(FP8X4),
-                            lhsT_scale=w2_q[a][1][:, P * t : P * (t + 1)],
+                            w2_sums[:, u, :],
+                            lhsT=codes[:, P * u : P * (u + 1)].bitcast(FP8X4),
+                            lhsT_scale=plane[:, P * u : P * (u + 1)],
                             rhs=v_codes[a][:, cols].bitcast(FP8X4),
                             rhs_scale=v_plane[:, a, cols],
                             start=(a == 0 and u == 0),
-                            stop=(a == passes - 1 and u == 1),
+                            stop=(a == PASSES - 1 and u == PAIR - 1),
                         )
-                left_sb = both_sb[:, 2 * half : 2 * half + 2, :]
-                nc.scalar.copy(left_sb, left[:])
-                for u in range(2):
-                    nc.vector.tensor_tensor(h1[2 * half + u][:, cols], right[:, u, :], left_sb[:, u, :], MULT)
+                staged = w1_sums_sb[:, PAIR * pair : PAIR * (pair + 1), :]
+                nc.scalar.copy(staged, w1_sums[:])
+                for u in range(PAIR):
+                    nc.vector.tensor_tensor(h1[PAIR * pair + u][:, cols], w2_sums[:, u, :], staged[:, u, :], MULT)
 
-        def gain_round_quantize(name, values, width, slot):
-            planar = ring.tile([P, PACK, width], BF16, tag=slot, bufs=1, name="planar")
+        def grouped_tile(width):
+            return ring.tile([P, PACK * width], BF16, tag="grouped", bufs=2, name="grouped", align_bytes=64)
+
+        def gain_round_quantize(name, values, tag):
+            width = values.shape[2]
+            planar = ring.tile([P, PACK, width], BF16, tag=tag, name="planar")
             for t in range(PACK):
-                nc.scalar.activation(planar[:, t, :], values[t], COPY, scale=gr_sb[:, t : t + 1])
-            grouped = ring.tile([P, PACK * width], BF16, tag="grouped", name="grouped", align_bytes=64)
-            interleave(grouped, planar, 0, width)
-            return quantize(name, grouped[:], width)
+                nc.scalar.activation(planar[:, t, :], values[:, t, :], COPY, scale=gr_sb[:, t : t + 1])
+            grouped = grouped_tile(width)
+            nc.scalar.copy(interleaved_view(grouped), planar_view(planar[:]))
+            return quantize(name, grouped, width)
+
+        def tanh_chunk(c):
+            tanh_h1 = ring.tile([P, PACK, CHUNK], F32, tag="tanh_h1", bufs=2, name="tanh_h1")
+            for t in range(PACK):
+                nc.scalar.activation(tanh_h1[:, t, :], h1[t][:, chunk_columns(c)], TANH)
+            return tanh_h1
+
+        def z1_first_chunk():
+            tanh_h1 = tanh_chunk(0)
+            grouped = grouped_tile(CHUNK)
+            gain = gr_sb[:].unsqueeze(1).unsqueeze(3).to_broadcast([P, CHUNK // RUN, PACK, RUN])
+            nc.vector.tensor_tensor(interleaved_view(grouped), planar_view(tanh_h1[:]), gain, MULT)
+            return quantize("z1_0", grouped, CHUNK)
 
         def z1_chunk(c):
-            cols = slice(c * CHUNK, (c + 1) * CHUNK)
-            bent = ring.tile([P, PACK, CHUNK], F32, tag="bent", name="bent")
-            for t in range(PACK):
-                nc.scalar.activation(bent[:, t, :], h1[t][:, cols], TANH)
-            if c == 0:
-                grouped = ring.tile([P, PACK * CHUNK], BF16, tag="grouped", name="grouped", align_bytes=64)
-                nc.vector.tensor_tensor(
-                    grouped[:].rearrange("p (c i j) -> p c j i", i=4, j=PACK),
-                    bent[:].rearrange("p j (c i) -> p c j i", i=4),
-                    gr_sb[:].unsqueeze(1).unsqueeze(3).to_broadcast([P, CHUNK // 4, PACK, 4]),
-                    MULT,
-                )
-                return quantize("z1_0", grouped[:], CHUNK)
-            return gain_round_quantize("z1_%d" % c, [bent[:, t, :] for t in range(PACK)], CHUNK, "handover")
+            return gain_round_quantize("z1_%d" % c, tanh_chunk(c)[:], "after_z1")
 
-        def second_stage(n, z_q, weight, weight_plane, gains, entries, slot):
+        def second_stage(n, z_q, weight, weight_plane, gains, entries, after):
+            codes, plane = z_q
             width = gains.shape[1]
             y = psum.tile([P, width], F32, tag="y", bufs=2, name="y")
             nc.tensor.matmul_mx(
                 y[:], lhsT=weight, lhsT_scale=weight_plane,
-                rhs=z_q[0][:].bitcast(FP8X4), rhs_scale=z_q[1][:], start=True, stop=True,
+                rhs=codes[:].bitcast(FP8X4), rhs_scale=plane[:], start=True, stop=True,
             )
-            y_sb = ring.tile([P, width], F32, tag=slot, bufs=3 if slot == "y_sb" else 1, name=slot)
+            if after is None:
+                y_sb = ring.tile([P, width], F32, tag="y_sb", bufs=ROW_TILES, name="y_sb")
+            else:
+                y_sb = ring.tile([P, width], F32, tag=after, name="y_held")
             nc.scalar.copy(y_sb[:], y[:])
             nc.vector.tensor_tensor(page[n][:].indirect(entries), y_sb[:], gains, MULT)
 
-        def y1_tile(c, n, slot="y_sb"):
+        def y1_tile(c, n, after=None):
+            codes, plane = w5_q[n]
             second_stage(
-                n, z1_q[c], w5_q[n][0][:].bitcast(FP8X4), w5_q[n][1][:],
-                wg1_sb[:, c * CHUNK : (c + 1) * CHUNK],
-                offs3_sb[:, c * CHUNK // STRIPE : (c + 1) * CHUNK // STRIPE], slot,
+                n, z1_q[c], codes[:].bitcast(FP8X4), plane[:],
+                wg1_sb[:, chunk_columns(c)], chunk_entries(offs3_sb, c), after,
             )
-
-        def quantize_w5(n):
-            raw = w5_first[:] if n == 0 else w5_rest[:, :, P * (n - 1) : P * n]
-            grouped = held("w5_grouped%d" % n, [P, PACK * P], BF16)
-            nc.scalar.copy(
-                grouped[:].rearrange("p (c i j) -> p c j i", i=4, j=PACK),
-                raw.rearrange("p j (c i) -> p c j i", i=4),
-            )
-            return quantize("w5_%d" % n, grouped[:], P)
 
         z1_q = [None] * CHUNKS
         w5_q = [None] * ROW_TILES
         w5_q[0] = quantize_w5(0)
         first_stage(0)
-        z1_q[0] = z1_chunk(0)
+        z1_q[0] = z1_first_chunk()
         first_stage(1)
         w5_q[1] = quantize_w5(1)
         y1_tile(0, 0)
@@ -268,21 +284,21 @@ def tile_list_repatriation_reserve_features_kernel(
         first_stage(2)
         first_stage(3)
         z1_q[1] = z1_chunk(1)
-        y1_tile(0, 2, "handover")
+        y1_tile(0, 2, "after_z1")
         y1_tile(1, 0)
         y1_tile(1, 1)
         z1_q[2] = z1_chunk(2)
-        y1_tile(1, 2, "handover")
+        y1_tile(1, 2, "after_z1")
         y1_tile(2, 0)
 
-        w3_q = quantize_dealt("w3", w3_raw, 4, 0)
+        w3_q = [quantize_dealt_pair("w3_%d" % pair, w3_raw, pair, nc.scalar.copy, 2) for pair in range(PAIRS)]
         z1_q[3] = z1_chunk(3)
         v2_codes = held("v2_codes", [P, C], U32)
         v2_plane = held("v2_plane", [P, C], U8)
         nc.vector.tensor_copy(v2_codes[:], tab2_sb[:].bitcast(U32).indirect(offs2_sb[:]))
         nc.vector.tensor_copy(v2_plane[:], tab2_plane[:, 0, :].indirect(offs2_sb[:]))
+        y1_tile(2, 1, "after_tab2")
 
-        y1_tile(2, 1, "tab2_slot")
         w4_codes = held("w4_codes", [P, H], U32)
         nc.scalar.copy(
             w4_codes[:].rearrange("p (t m) -> p m t", t=PACK),
@@ -293,35 +309,37 @@ def tile_list_repatriation_reserve_features_kernel(
             w4_plane[:].rearrange("p (t m) -> p t m", t=PACK),
             w4_plane_raw[:, 0, :].rearrange("p (m t) -> p t m", t=PACK),
         )
-        h2 = [ring.tile([P, C], F32, tag="h2_%d" % t, bufs=1, name="h2") for t in range(PACK)]
+        h2 = [ring.tile([P, C], F32, tag="after_h2_%d" % t, name="h2") for t in range(PACK)]
         for t in range(PACK):
-            left = psum.tile([P, C], F32, tag="left", bufs=3, name="left")
-            right = psum.tile([P, C], F32, tag="right", bufs=3, name="right")
-            cols = slice(P * t, P * (t + 1))
+            w3_sums = psum.tile([P, C], F32, tag="left", bufs=3, name="w3_sums")
+            w4_sums = psum.tile([P, C], F32, tag="right", bufs=3, name="w4_sums")
+            codes, plane = w3_q[t // PAIR]
+            in_pair = slice(P * (t % PAIR), P * (t % PAIR + 1))
+            in_all = slice(P * t, P * (t + 1))
             nc.tensor.matmul_mx(
-                left[:], lhsT=w3_q[0][:, cols].bitcast(FP8X4), lhsT_scale=w3_q[1][:, cols],
+                w3_sums[:], lhsT=codes[:, in_pair].bitcast(FP8X4), lhsT_scale=plane[:, in_pair],
                 rhs=v2_codes[:].bitcast(FP8X4), rhs_scale=v2_plane[:], start=True, stop=True,
             )
             nc.tensor.matmul_mx(
-                right[:], lhsT=w4_codes[:, cols].bitcast(FP8X4), lhsT_scale=w4_plane[:, cols],
+                w4_sums[:], lhsT=w4_codes[:, in_all].bitcast(FP8X4), lhsT_scale=w4_plane[:, in_all],
                 rhs=v2_codes[:].bitcast(FP8X4), rhs_scale=v2_plane[:], start=True, stop=True,
             )
-            left_sb = ring.tile([P, C], F32, tag="left_sb", bufs=2, name="left_sb")
-            nc.scalar.copy(left_sb[:], left[:])
-            nc.vector.tensor_tensor(h2[t][:], right[:], left_sb[:], MULT)
+            w3_sums_sb = ring.tile([P, C], F32, tag="w3_sums_sb", bufs=2, name="w3_sums_sb")
+            nc.scalar.copy(w3_sums_sb[:], w3_sums[:])
+            nc.vector.tensor_tensor(h2[t][:], w4_sums[:], w3_sums_sb[:], MULT)
 
         joined = held("joined", [P, PACK, C], F32)
         for t in range(PACK):
             nc.vector.tensor_tensor(joined[:, t, :], h1[t][:].indirect(pos1_sb[:]), h2[t][:], ADD)
-        y1_tile(2, 2, "h2_0")
-        y1_tile(3, 0, "h2_1")
-        y1_tile(3, 1, "h2_2")
-        z2_q = gain_round_quantize("z2", [joined[:, t, :] for t in range(PACK)], C, "last_handover")
-        y1_tile(3, 2, "last_handover")
+        y1_tile(2, 2, "after_h2_0")
+        y1_tile(3, 0, "after_h2_1")
+        y1_tile(3, 1, "after_h2_2")
+        z2_q = gain_round_quantize("z2", joined[:], "after_z2")
+        y1_tile(3, 2, "after_z2")
         for n in range(ROW_TILES):
             second_stage(
                 n, z2_q, w6_sb[:, 2 * P * n : 2 * P * (n + 1)].bitcast(FP4X4), w6_plane[:, 0, P * n : P * (n + 1)],
-                wg2_sb[:], offs4_sb[:], "y_sb",
+                wg2_sb[:], offs4_sb[:], None,
             )
         for n in range(ROW_TILES):
             nc.sync.dma_start(out[n * P : (n + 1) * P, :], page[n][:])

from contextlib import ExitStack

import concourse.mybir as mybir

K, R, H, N, T, S, C = 1024, 512, 512, 384, 2048, 1024, 512
FLOPS = 2 * (2 * K * H * S + 2 * R * H * C + H * N * (S + C))

F32 = mybir.dt.float32
BF16 = mybir.dt.bfloat16
I32 = mybir.dt.int32
U32 = mybir.dt.uint32
U16 = mybir.dt.uint16
U8 = mybir.dt.uint8
FP8X4 = mybir.dt.float8_e4m3fn_x4
FP4X4 = mybir.dt.float4_e2m1fn_x4
MULT = mybir.AluOpType.mult
ADD = mybir.AluOpType.add
TANH = mybir.ActivationFunctionType.Tanh
COPY = mybir.ActivationFunctionType.Copy

P = 128
PACK = 4
K_PASS = P * PACK
PASSES = K // K_PASS
QUADRANT = 32
QUADRANTS = P // QUADRANT
SCALE_ROWS = 4
PAIR = 2
PAIRS = PACK // PAIR
CHUNK = 256
CHUNKS = S // CHUNK
ROW_TILES = N // P
STRIPE = 16
RUN = 4


def tile_list_repatriation_reserve_features_kernel(
    tc, tab_words, tab_scales, tab2_words, tab2_scales, offs, offs2, pos1, offs3, offs4,
    w1_words, w1_scales, w2, w3, w4_words, w4_scales, gr, w5, w6_words, w6_scales,
    page1, wg1, wg2, out,
):
    nc = tc.nc

    with ExitStack() as ctx:
        keep = ctx.enter_context(tc.tile_pool(name="keep", bufs=1))
        ring = ctx.enter_context(tc.tile_pool(name="ring", bufs=1))
        psum = ctx.enter_context(tc.psum_pool(name="psum", bufs=1))

        def held(name, shape, dtype):
            return keep.tile(shape, dtype, name=name, align_bytes=64)

        def load_list(name, src):
            tile = keep.tile(list(src.shape), U16, name=name)
            nc.sync.dma_start(tile[:], src)
            return tile

        def load(name, src, dtype):
            tile = held(name, list(src.shape), dtype)
            nc.sync.dma_start(tile[:], src)
            return tile

        def zeroed_planes(name, passes, columns):
            tile = held(name, [P, passes, columns], U8)
            nc.gpsimd.memset(tile[:].bitcast(I32), 0)
            return tile

        def load_planes(tile, scales):
            for q in range(QUADRANTS):
                nc.sync.dma_start(
                    tile[QUADRANT * q : QUADRANT * q + SCALE_ROWS, :, :].bitcast(I32),
                    scales[:, SCALE_ROWS * q : SCALE_ROWS * (q + 1), :].rearrange("a r c -> r a c").bitcast(I32),
                )

        def as_words(src):
            return src.rearrange("p c i -> p (c i)").bitcast(I32)

        def four_rows_a_partition(src):
            return src.rearrange("(p j) c -> p j c", j=PACK)

        def chunk_columns(c):
            return slice(c * CHUNK, (c + 1) * CHUNK)

        def chunk_entries(list_tile, c):
            return list_tile[:, c * CHUNK // STRIPE : (c + 1) * CHUNK // STRIPE]

        tab_rows = held("tab_rows", [P, T], U8)
        nc.vector.memset(tab_rows[QUADRANT : 2 * QUADRANT, :].bitcast(I32), 0)
        nc.vector.memset(tab_rows[2 * QUADRANT :, :].bitcast(I32), 0)
        w1_plane_raw = zeroed_planes("w1_plane_raw", PASSES, H)
        v_plane = zeroed_planes("v_plane", PASSES, S)
        tab2_plane = zeroed_planes("tab2_plane", 1, T)
        w4_plane_raw = zeroed_planes("w4_plane_raw", 1, H)
        w6_plane = zeroed_planes("w6_plane", 1, N)

        nc.sync.dma_start(tab_rows[:QUADRANT, :].bitcast(I32), tab_scales.rearrange("a g t -> g a t").bitcast(I32))
        offs_sb = load_list("offs_sb", offs)
        tab_pass0 = load("tab_pass0", as_words(tab_words[0]), I32)
        w1_raw = held("w1_raw", [P, PASSES, 2 * H], U8)
        nc.sync.dma_start(w1_raw[:].bitcast(I32), w1_words.rearrange("a p c -> p a c").bitcast(I32))
        load_planes(w1_plane_raw, w1_scales)
        tab_pass1 = load("tab_pass1", as_words(tab_words[1]), I32)

        v_rows = held("v_rows", [P, S], U8)
        nc.vector.tensor_copy(v_rows[:], tab_rows[:].indirect(offs_sb[:]))
        rows_a_quadrant = SCALE_ROWS * PASSES
        for q in range(QUADRANTS):
            nc.sync.dma_start(
                v_plane[QUADRANT * q : QUADRANT * q + SCALE_ROWS, :, :].bitcast(I32),
                v_rows[rows_a_quadrant * q : rows_a_quadrant * (q + 1), :].bitcast(I32),
            )

        w2_raw = [ring.tile([P, PACK, H], F32, tag="after_w2", bufs=PASSES, name="w2_raw") for a in range(PASSES)]
        for a in range(PASSES):
            nc.sync.dma_start(w2_raw[a][:], four_rows_a_partition(w2[a * K_PASS : (a + 1) * K_PASS, :]))
        w5_first = load("w5_first", four_rows_a_partition(w5[:, :P]), F32)
        gr_sb = load("gr_sb", gr.rearrange("(p t) -> p t", t=PACK), F32)
        offs3_sb = load_list("offs3_sb", offs3)
        wg1_sb = load("wg1_sb", wg1, F32)
        w5_rest = load("w5_rest", four_rows_a_partition(w5[:, P:]), F32)
        page = [load("page%d" % n, page1[n * P : (n + 1) * P, :], F32) for n in range(ROW_TILES)]
        w3_raw = load("w3_raw", four_rows_a_partition(w3), F32)
        offs2_sb = load_list("offs2_sb", offs2)
        load_planes(tab2_plane, tab2_scales)
        tab2_sb = ring.tile([P, T], I32, tag="after_tab2", name="tab2_sb")
        nc.sync.dma_start(tab2_sb[:], as_words(tab2_words[0]))
        w4_raw = load("w4_raw", as_words(w4_words[0]), I32)
        load_planes(w4_plane_raw, w4_scales)
        pos1_sb = load_list("pos1_sb", pos1)
        offs4_sb = load_list("offs4_sb", offs4)
        wg2_sb = load("wg2_sb", wg2, F32)
        w6_sb = held("w6_sb", [P, 2 * N], U8)
        nc.sync.dma_start(w6_sb[:].bitcast(I32), w6_words[0].bitcast(I32))
        load_planes(w6_plane, w6_scales)

        def quantize(name, grouped, width):
            codes = held(name + "_codes", [P, width], U32)
            plane = held(name + "_plane", [P, width], U8)
            nc.vector.quantize_mx(out=codes[:].bitcast(FP8X4), scales=plane[:], in_=grouped[:])
            return codes, plane

        def interleaved_view(grouped):
            return grouped[:].rearrange("p (c i j) -> p c j i", i=RUN, j=PACK)

        def planar_view(planar):
            return planar.rearrange("p j (c i) -> p c j i", i=RUN)

        def quantize_dealt_pair(name, raw, pair, copy, pieces):
            grouped = held(name + "_grouped", [P, PACK * PAIR * P], BF16)
            dst = grouped[:].rearrange("p (u m j) -> p m j u", u=PAIR, j=PACK)
            src = raw[:].rearrange("p j (m t) -> p m j t", t=PACK)[:, :, :, PAIR * pair : PAIR * (pair + 1)]
            step = P // pieces
            for m0 in range(0, P, step):
                copy(dst[:, m0 : m0 + step], src[:, m0 : m0 + step])
            return quantize(name, grouped, PAIR * P)

        def quantize_w5(n):
            raw = w5_first[:] if n == 0 else w5_rest[:, :, P * (n - 1) : P * n]
            grouped = held("w5_grouped%d" % n, [P, PACK * P], BF16)
            nc.scalar.copy(interleaved_view(grouped), planar_view(raw))
            return quantize("w5_%d" % n, grouped, P)

        v_codes = [held("v_codes%d" % a, [P, S], U32) for a in range(PASSES)]
        nc.vector.tensor_copy(v_codes[0][:], tab_pass0[:].bitcast(U32).indirect(offs_sb[:]))
        w1_codes = held("w1_codes", [P, PASSES, 2 * H], U8)
        nc.scalar.copy(
            w1_codes[:].bitcast(U16).rearrange("p a (t m) -> p a t m", t=PACK),
            w1_raw[:].bitcast(U16).rearrange("p a (m t) -> p a t m", t=PACK),
        )
        w1_plane = held("w1_plane", [P, PASSES, H], U8)
        nc.gpsimd.tensor_copy(
            w1_plane[:].rearrange("p a (t m) -> p a t m", t=PACK),
            w1_plane_raw[:].rearrange("p a (m t) -> p a t m", t=PACK),
        )
        for c in range(CHUNKS):
            nc.vector.tensor_copy(
                v_codes[1][:, chunk_columns(c)], tab_pass1[:].bitcast(U32).indirect(chunk_entries(offs_sb, c))
            )
        w2_copies = (
            (nc.vector.tensor_copy, nc.scalar.copy),
            (nc.vector.tensor_copy, nc.vector.tensor_copy),
        )
        w2_q = [
            [quantize_dealt_pair("w2_%d_%d" % (a, pair), w2_raw[a], pair, w2_copies[a][pair], 1) for pair in range(PAIRS)]
            for a in range(PASSES)
        ]

        h1 = [held("h1_%d" % t, [P, S], F32) for t in range(PACK)]

        def first_stage(c):
            cols = chunk_columns(c)
            w1_sums_sb = ring.tile([P, PACK, CHUNK], F32, tag="after_w2", bufs=PASSES, name="w1_sums_sb")
            for pair in range(PAIRS):
                w1_sums = psum.tile([P, PAIR, CHUNK], F32, tag="left", bufs=3, name="w1_sums")
                w2_sums = psum.tile([P, PAIR, CHUNK], F32, tag="right", bufs=3, name="w2_sums")
                for a in range(PASSES):
                    for u in range(PAIR):
                        t = PAIR * pair + u
                        nc.tensor.matmul_mx(
                            w1_sums[:, u, :],
                            lhsT=w1_codes[:, a, 2 * P * t : 2 * P * (t + 1)].bitcast(FP4X4),
                            lhsT_scale=w1_plane[:, a, P * t : P * (t + 1)],
                            rhs=v_codes[a][:, cols].bitcast(FP8X4),
                            rhs_scale=v_plane[:, a, cols],
                            start=(a == 0 and u == 0),
                            stop=(a == PASSES - 1 and u == PAIR - 1),
                        )
                for a in range(PASSES):
                    codes, plane = w2_q[a][pair]
                    for u in range(PAIR):
                        nc.tensor.matmul_mx(
                            w2_sums[:, u, :],
                            lhsT=codes[:, P * u : P * (u + 1)].bitcast(FP8X4),
                            lhsT_scale=plane[:, P * u : P * (u + 1)],
                            rhs=v_codes[a][:, cols].bitcast(FP8X4),
                            rhs_scale=v_plane[:, a, cols],
                            start=(a == 0 and u == 0),
                            stop=(a == PASSES - 1 and u == PAIR - 1),
                        )
                staged = w1_sums_sb[:, PAIR * pair : PAIR * (pair + 1), :]
                nc.scalar.copy(staged, w1_sums[:])
                for u in range(PAIR):
                    nc.vector.tensor_tensor(h1[PAIR * pair + u][:, cols], w2_sums[:, u, :], staged[:, u, :], MULT)

        def grouped_tile(width):
            return ring.tile([P, PACK * width], BF16, tag="grouped", bufs=2, name="grouped", align_bytes=64)

        def gain_round_quantize(name, values, tag):
            width = values.shape[2]
            planar = ring.tile([P, PACK, width], BF16, tag=tag, name="planar")
            for t in range(PACK):
                nc.scalar.activation(planar[:, t, :], values[:, t, :], COPY, scale=gr_sb[:, t : t + 1])
            grouped = grouped_tile(width)
            nc.scalar.copy(interleaved_view(grouped), planar_view(planar[:]))
            return quantize(name, grouped, width)

        def tanh_chunk(c):
            tanh_h1 = ring.tile([P, PACK, CHUNK], F32, tag="tanh_h1", bufs=2, name="tanh_h1")
            for t in range(PACK):
                nc.scalar.activation(tanh_h1[:, t, :], h1[t][:, chunk_columns(c)], TANH)
            return tanh_h1

        def z1_first_chunk():
            tanh_h1 = tanh_chunk(0)
            grouped = grouped_tile(CHUNK)
            gain = gr_sb[:].unsqueeze(1).unsqueeze(3).to_broadcast([P, CHUNK // RUN, PACK, RUN])
            nc.vector.tensor_tensor(interleaved_view(grouped), planar_view(tanh_h1[:]), gain, MULT)
            return quantize("z1_0", grouped, CHUNK)

        def z1_chunk(c):
            return gain_round_quantize("z1_%d" % c, tanh_chunk(c)[:], "after_z1")

        def second_stage(n, z_q, weight, weight_plane, gains, entries, after):
            codes, plane = z_q
            width = gains.shape[1]
            y = psum.tile([P, width], F32, tag="y", bufs=2, name="y")
            nc.tensor.matmul_mx(
                y[:], lhsT=weight, lhsT_scale=weight_plane,
                rhs=codes[:].bitcast(FP8X4), rhs_scale=plane[:], start=True, stop=True,
            )
            if after is None:
                y_sb = ring.tile([P, width], F32, tag="y_sb", bufs=ROW_TILES, name="y_sb")
            else:
                y_sb = ring.tile([P, width], F32, tag=after, name="y_held")
            nc.scalar.copy(y_sb[:], y[:])
            nc.vector.tensor_tensor(page[n][:].indirect(entries), y_sb[:], gains, MULT)

        def y1_tile(c, n, after=None):
            codes, plane = w5_q[n]
            second_stage(
                n, z1_q[c], codes[:].bitcast(FP8X4), plane[:],
                wg1_sb[:, chunk_columns(c)], chunk_entries(offs3_sb, c), after,
            )

        z1_q = [None] * CHUNKS
        w5_q = [None] * ROW_TILES
        w5_q[0] = quantize_w5(0)
        first_stage(0)
        z1_q[0] = z1_first_chunk()
        first_stage(1)
        w5_q[1] = quantize_w5(1)
        y1_tile(0, 0)
        w5_q[2] = quantize_w5(2)
        y1_tile(0, 1)
        first_stage(2)
        first_stage(3)
        z1_q[1] = z1_chunk(1)
        y1_tile(0, 2, "after_z1")
        y1_tile(1, 0)
        y1_tile(1, 1)
        z1_q[2] = z1_chunk(2)
        y1_tile(1, 2, "after_z1")
        y1_tile(2, 0)

        w3_q = [quantize_dealt_pair("w3_%d" % pair, w3_raw, pair, nc.scalar.copy, 2) for pair in range(PAIRS)]
        z1_q[3] = z1_chunk(3)
        v2_codes = held("v2_codes", [P, C], U32)
        v2_plane = held("v2_plane", [P, C], U8)
        nc.vector.tensor_copy(v2_codes[:], tab2_sb[:].bitcast(U32).indirect(offs2_sb[:]))
        nc.vector.tensor_copy(v2_plane[:], tab2_plane[:, 0, :].indirect(offs2_sb[:]))
        y1_tile(2, 1, "after_tab2")

        w4_codes = held("w4_codes", [P, H], U32)
        nc.scalar.copy(
            w4_codes[:].rearrange("p (t m) -> p m t", t=PACK),
            w4_raw[:].bitcast(U32).rearrange("p (m t) -> p m t", t=PACK),
        )
        w4_plane = held("w4_plane", [P, H], U8)
        nc.gpsimd.tensor_copy(
            w4_plane[:].rearrange("p (t m) -> p t m", t=PACK),
            w4_plane_raw[:, 0, :].rearrange("p (m t) -> p t m", t=PACK),
        )
        h2 = [ring.tile([P, C], F32, tag="after_h2_%d" % t, name="h2") for t in range(PACK)]
        for t in range(PACK):
            w3_sums = psum.tile([P, C], F32, tag="left", bufs=3, name="w3_sums")
            w4_sums = psum.tile([P, C], F32, tag="right", bufs=3, name="w4_sums")
            codes, plane = w3_q[t // PAIR]
            in_pair = slice(P * (t % PAIR), P * (t % PAIR + 1))
            in_all = slice(P * t, P * (t + 1))
            nc.tensor.matmul_mx(
                w3_sums[:], lhsT=codes[:, in_pair].bitcast(FP8X4), lhsT_scale=plane[:, in_pair],
                rhs=v2_codes[:].bitcast(FP8X4), rhs_scale=v2_plane[:], start=True, stop=True,
            )
            nc.tensor.matmul_mx(
                w4_sums[:], lhsT=w4_codes[:, in_all].bitcast(FP8X4), lhsT_scale=w4_plane[:, in_all],
                rhs=v2_codes[:].bitcast(FP8X4), rhs_scale=v2_plane[:], start=True, stop=True,
            )
            w3_sums_sb = ring.tile([P, C], F32, tag="w3_sums_sb", bufs=2, name="w3_sums_sb")
            nc.scalar.copy(w3_sums_sb[:], w3_sums[:])
            nc.vector.tensor_tensor(h2[t][:], w4_sums[:], w3_sums_sb[:], MULT)

        joined = held("joined", [P, PACK, C], F32)
        for t in range(PACK):
            nc.vector.tensor_tensor(joined[:, t, :], h1[t][:].indirect(pos1_sb[:]), h2[t][:], ADD)
        y1_tile(2, 2, "after_h2_0")
        y1_tile(3, 0, "after_h2_1")
        y1_tile(3, 1, "after_h2_2")
        z2_q = gain_round_quantize("z2", joined[:], "after_z2")
        y1_tile(3, 2, "after_z2")
        for n in range(ROW_TILES):
            second_stage(
                n, z2_q, w6_sb[:, 2 * P * n : 2 * P * (n + 1)].bitcast(FP4X4), w6_plane[:, 0, P * n : P * (n + 1)],
                wg2_sb[:], offs4_sb[:], None,
            )
        for n in range(ROW_TILES):
            nc.sync.dma_start(out[n * P : (n + 1) * P, :], page[n][:])
